import numpy as np
import ml_dtypes

BF16 = ml_dtypes.bfloat16


def bf(x):
    return np.asarray(x, np.float32).astype(BF16)


def f32(x):
    return np.asarray(x, np.float32)


def f64(x):
    return np.asarray(x).astype(np.float64)


def striped(idx):
    return np.tile(idx.reshape(-1, 16).T, (8, 1))


def rows(idx, k):
    return np.tile(idx, (k, 1))


def look(tab, idx):
    return np.take_along_axis(f64(tab), rows(idx, len(tab)), axis=1)


K, S, H, D, V, N, M = 256, 2048, 256, 2, 512, 1024, 256


def setup_inputs():
    return {"z": bf(np.random.standard_normal((H, S))), "wt": bf(np.random.standard_normal((H, K)) / np.sqrt(H)), "x0": f32(1.0 * np.random.standard_normal((K, V))), "w": bf(np.random.standard_normal((K, M)) / np.sqrt(K)), "b": f32(0.5 * np.random.standard_normal((M, 1))), "offs": striped(np.random.permutation(S)[:N])}


def reference(z, wt, x0, w, b, offs):
    idx = offs[:16].T.reshape(-1)
    tab = f64(wt).T @ f64(z)
    x = f64(x0)
    for d in range(D):
        x = np.maximum(x, look(tab, idx[d * V:(d + 1) * V]))
    return np.maximum(f64(w).T @ x + f64(b), 0.0)

@@ -1,0 +1,84 @@
+import concourse.mybir as mybir
+
+BF16, F32, U16 = mybir.dt.bfloat16, mybir.dt.float32, mybir.dt.uint16
+MAX = mybir.AluOpType.max
+RELU = mybir.ActivationFunctionType.Relu
+
+P = 128
+BANK = 512
+LANES = 16
+PIECE = 256
+
+FLOPS = 2 * 256 * 256 * 2048 + 2 * 256 * 256 * 512
+
+
+def tile_lookup_pjmax_relu_kernel(tc, z, wt, x0, w, b, offs, out):
+    nc = tc.nc
+    features, places = z.shape
+    rows, nodes = x0.shape
+    outputs = w.shape[1]
+    k_blocks, r_blocks, m_blocks = features // P, rows // P, outputs // P
+    chunks, pieces = places // BANK, nodes // PIECE
+    neighbours = offs.shape[1] * LANES // nodes
+
+    with (
+        tc.tile_pool(name="held", bufs=1) as held,
+        tc.psum_pool(name="psum", bufs=8) as psum,
+    ):
+        offsets = held.tile([P, offs.shape[1]], U16, name="offsets")
+        wt_sb = held.tile([P, k_blocks, rows], BF16, name="wt_sb")
+        z_sb = [held.tile([P, k_blocks, BANK], BF16, name=f"z{c}") for c in range(chunks)]
+        x0_sb = [held.tile([P, nodes], F32, name=f"x0_{r}") for r in range(r_blocks)]
+        w_sb = held.tile([P, r_blocks, outputs], BF16, name="w_sb")
+        bias = [held.tile([P, 1], F32, name=f"bias{m}") for m in range(m_blocks)]
+
+        z_rows = z.rearrange("(p k) i -> p k i", k=k_blocks)
+        nc.sync.dma_start(wt_sb[:], wt.rearrange("(p k) r -> p k r", k=k_blocks))
+        for c in range(chunks):
+            nc.sync.dma_start(z_sb[c][:], z_rows[:, :, c * BANK:(c + 1) * BANK])
+        nc.sync.dma_start(offsets[:], offs)
+        for r in range(r_blocks):
+            nc.sync.dma_start(x0_sb[r][:], x0[r * P:(r + 1) * P, :])
+        nc.sync.dma_start(w_sb[:], w.rearrange("(r p) m -> p r m", p=P))
+        for m in range(m_blocks):
+            nc.sync.dma_start(bias[m][:], b[m * P:(m + 1) * P, :])
+
+        tab = [held.tile([P, places], F32, name=f"tab{r}") for r in range(r_blocks)]
+        for r in range(r_blocks):
+            for c in range(chunks):
+                bank = psum.tile([P, BANK], F32, name="bank")
+                for k in range(k_blocks):
+                    nc.tensor.matmul(bank[:], wt_sb[:, k, r * P:(r + 1) * P], z_sb[c][:, k, :],
+                                     start=(k == 0), stop=(k == k_blocks - 1))
+                columns = tab[r][:, c * BANK:(c + 1) * BANK]
+                if r == 0:
+                    nc.vector.tensor_copy(columns, bank[:])
+                else:
+                    nc.scalar.copy(columns, bank[:])
+
+        x_bf = [held.tile([P, nodes], BF16, name=f"x_bf{r}") for r in range(r_blocks)]
+        for r in range(r_blocks):
+            best = x0_sb[r]
+            for d in range(neighbours):
+                larger = held.tile([P, nodes], F32, name=f"larger{r}_{d}")
+                for h in range(pieces):
+                    first = (d * nodes + h * PIECE) // LANES
+                    picked = tab[r][:].indirect(offsets[:, first:first + PIECE // LANES])
+                    js = slice(h * PIECE, (h + 1) * PIECE)
+                    nc.vector.tensor_tensor(larger[:, js], picked, best[:, js], MAX)
+                best = larger
+            for h in range(pieces):
+                js = slice(h * PIECE, (h + 1) * PIECE)
+                nc.scalar.copy(x_bf[r][:, js], best[:, js])
+
+        out_rows = out.rearrange("(m p) j -> p m j", p=P)
+        for h in range(pieces):
+            js = slice(h * PIECE, (h + 1) * PIECE)
+            result = held.tile([P, m_blocks, PIECE], F32, name=f"result{h}")
+            for m in range(m_blocks):
+                bank = psum.tile([P, BANK], F32, name="bank")
+                for r in range(r_blocks):
+                    nc.tensor.matmul(bank[:, :PIECE], w_sb[:, r, m * P:(m + 1) * P], x_bf[r][:, js],
+                                     start=(r == 0), stop=(r == r_blocks - 1))
+                nc.scalar.activation(result[:, m, :], bank[:, :PIECE], RELU, bias=bias[m][:])
+            nc.sync.dma_start(out_rows[:, :, js], result[:])

@@ -1,13 +1,14 @@
 import concourse.mybir as mybir
 
 BF16, F32, U16 = mybir.dt.bfloat16, mybir.dt.float32, mybir.dt.uint16
-MAX = mybir.AluOpType.max
+ADD, MAX = mybir.AluOpType.add, mybir.AluOpType.max
 RELU = mybir.ActivationFunctionType.Relu
 
 P = 128
 BANK = 512
 LANES = 16
-PIECE = 256
+HALF = 256
+WARM_UPS = 8
 
 FLOPS = 2 * 256 * 256 * 2048 + 2 * 256 * 256 * 512
 
@@ -18,7 +19,9 @@ def tile_lookup_pjmax_relu_kernel(tc, z, wt, x0, w, b, offs, out):
     rows, nodes = x0.shape
     outputs = w.shape[1]
     k_blocks, r_blocks, m_blocks = features // P, rows // P, outputs // P
-    chunks, pieces = places // BANK, nodes // PIECE
+    halves = nodes // HALF
+    starts = list(range(0, places - BANK, BANK)) + [places - BANK, places - BANK // 2]
+    chunks = [slice(a, e) for a, e in zip(starts, starts[1:] + [places])]
     neighbours = offs.shape[1] * LANES // nodes
 
     with (
@@ -27,15 +30,15 @@ def tile_lookup_pjmax_relu_kernel(tc, z, wt, x0, w, b, offs, out):
     ):
         offsets = held.tile([P, offs.shape[1]], U16, name="offsets")
         wt_sb = held.tile([P, k_blocks, rows], BF16, name="wt_sb")
-        z_sb = [held.tile([P, k_blocks, BANK], BF16, name=f"z{c}") for c in range(chunks)]
+        z_sb = [held.tile([P, k_blocks, cols.stop - cols.start], BF16, name=f"z{c}") for c, cols in enumerate(chunks)]
         x0_sb = [held.tile([P, nodes], F32, name=f"x0_{r}") for r in range(r_blocks)]
         w_sb = held.tile([P, r_blocks, outputs], BF16, name="w_sb")
         bias = [held.tile([P, 1], F32, name=f"bias{m}") for m in range(m_blocks)]
 
         z_rows = z.rearrange("(p k) i -> p k i", k=k_blocks)
         nc.sync.dma_start(wt_sb[:], wt.rearrange("(p k) r -> p k r", k=k_blocks))
-        for c in range(chunks):
-            nc.sync.dma_start(z_sb[c][:], z_rows[:, :, c * BANK:(c + 1) * BANK])
+        for c, cols in enumerate(chunks):
+            nc.sync.dma_start(z_sb[c][:], z_rows[:, :, cols])
         nc.sync.dma_start(offsets[:], offs)
         for r in range(r_blocks):
             nc.sync.dma_start(x0_sb[r][:], x0[r * P:(r + 1) * P, :])
@@ -43,42 +46,55 @@ def tile_lookup_pjmax_relu_kernel(tc, z, wt, x0, w, b, offs, out):
         for m in range(m_blocks):
             nc.sync.dma_start(bias[m][:], b[m * P:(m + 1) * P, :])
 
+        zeros = held.tile([P, HALF], BF16, name="zeros")
+        nc.vector.memset(zeros[:], 0.0)
+        bank = psum.tile([P, BANK], F32, name="bank")
+        for i in range(WARM_UPS):
+            nc.tensor.matmul(bank[:, :HALF], zeros[:, :P], zeros[:], start=True, stop=True)
+
         tab = [held.tile([P, places], F32, name=f"tab{r}") for r in range(r_blocks)]
         for r in range(r_blocks):
-            for c in range(chunks):
+            for c, cols in enumerate(chunks):
                 bank = psum.tile([P, BANK], F32, name="bank")
+                projected = bank[:, :cols.stop - cols.start]
                 for k in range(k_blocks):
-                    nc.tensor.matmul(bank[:], wt_sb[:, k, r * P:(r + 1) * P], z_sb[c][:, k, :],
+                    nc.tensor.matmul(projected, wt_sb[:, k, r * P:(r + 1) * P], z_sb[c][:, k, :],
                                      start=(k == 0), stop=(k == k_blocks - 1))
-                columns = tab[r][:, c * BANK:(c + 1) * BANK]
-                if r == 0:
-                    nc.vector.tensor_copy(columns, bank[:])
+                if r == 0 and c % 2 == 0:
+                    nc.vector.tensor_copy(tab[r][:, cols], projected)
                 else:
-                    nc.scalar.copy(columns, bank[:])
+                    nc.scalar.copy(tab[r][:, cols], projected)
 
-        x_bf = [held.tile([P, nodes], BF16, name=f"x_bf{r}") for r in range(r_blocks)]
+        sums = {(h, m): psum.tile([P, BANK], F32, name="bank") for h in range(halves) for m in range(m_blocks)}
+        out_rows = out.rearrange("(m p) j -> p m j", p=P)
         for r in range(r_blocks):
             best = x0_sb[r]
             for d in range(neighbours):
                 larger = held.tile([P, nodes], F32, name=f"larger{r}_{d}")
-                for h in range(pieces):
-                    first = (d * nodes + h * PIECE) // LANES
-                    picked = tab[r][:].indirect(offsets[:, first:first + PIECE // LANES])
-                    js = slice(h * PIECE, (h + 1) * PIECE)
+                for h in range(halves):
+                    js = slice(h * HALF, (h + 1) * HALF)
+                    first = (d * nodes + h * HALF) // LANES
+                    picked = tab[r][:].indirect(offsets[:, first:first + HALF // LANES])
                     nc.vector.tensor_tensor(larger[:, js], picked, best[:, js], MAX)
                 best = larger
-            for h in range(pieces):
-                js = slice(h * PIECE, (h + 1) * PIECE)
-                nc.scalar.copy(x_bf[r][:, js], best[:, js])
-
-        out_rows = out.rearrange("(m p) j -> p m j", p=P)
-        for h in range(pieces):
-            js = slice(h * PIECE, (h + 1) * PIECE)
-            result = held.tile([P, m_blocks, PIECE], F32, name=f"result{h}")
-            for m in range(m_blocks):
-                bank = psum.tile([P, BANK], F32, name="bank")
-                for r in range(r_blocks):
-                    nc.tensor.matmul(bank[:, :PIECE], w_sb[:, r, m * P:(m + 1) * P], x_bf[r][:, js],
+            x_bf = held.tile([P, nodes], BF16, name=f"x_bf{r}")
+            for h in range(halves):
+                js = slice(h * HALF, (h + 1) * HALF)
+                last = r == r_blocks - 1 and h == halves - 1
+                if last:
+                    nc.vector.tensor_copy(x_bf[:, js], best[:, js])
+                else:
+                    nc.scalar.copy(x_bf[:, js], best[:, js])
+                for m in range(m_blocks):
+                    nc.tensor.matmul(sums[h, m][:, :HALF], w_sb[:, r, m * P:(m + 1) * P], x_bf[:, js],
                                      start=(r == 0), stop=(r == r_blocks - 1))
-                nc.scalar.activation(result[:, m, :], bank[:, :PIECE], RELU, bias=bias[m][:])
-            nc.sync.dma_start(out_rows[:, :, js], result[:])
+
+        for h in range(halves):
+            js = slice(h * HALF, (h + 1) * HALF)
+            for m in range(m_blocks):
+                result = held.tile([P, HALF], F32, name=f"result{h}_{m}")
+                if m % 2 == 1:
+                    nc.vector.tensor_scalar(result[:], sums[h, m][:, :HALF], bias[m][:], 0.0, ADD, MAX)
+                else:
+                    nc.scalar.activation(result[:], sums[h, m][:, :HALF], RELU, bias=bias[m][:])
+                nc.sync.dma_start(out_rows[:, m, js], result[:])

@@ -8,6 +8,7 @@ P = 128
 BANK = 512
 LANES = 16
 HALF = 256
+QUARTER = 128
 WARM_UPS = 8
 
 FLOPS = 2 * 256 * 256 * 2048 + 2 * 256 * 256 * 512
@@ -19,9 +20,9 @@ def tile_lookup_pjmax_relu_kernel(tc, z, wt, x0, w, b, offs, out):
     rows, nodes = x0.shape
     outputs = w.shape[1]
     k_blocks, r_blocks, m_blocks = features // P, rows // P, outputs // P
-    halves = nodes // HALF
     starts = list(range(0, places - BANK, BANK)) + [places - BANK, places - BANK // 2]
     chunks = [slice(a, e) for a, e in zip(starts, starts[1:] + [places])]
+    quarters = [slice(a, a + QUARTER) for a in range(0, nodes, QUARTER)]
     neighbours = offs.shape[1] * LANES // nodes
 
     with (
@@ -65,36 +66,35 @@ def tile_lookup_pjmax_relu_kernel(tc, z, wt, x0, w, b, offs, out):
                 else:
                     nc.scalar.copy(tab[r][:, cols], projected)
 
-        sums = {(h, m): psum.tile([P, BANK], F32, name="bank") for h in range(halves) for m in range(m_blocks)}
-        out_rows = out.rearrange("(m p) j -> p m j", p=P)
+        sums = [[psum.tile([P, QUARTER], F32, name="bank") for m in range(m_blocks)] for js in quarters]
         for r in range(r_blocks):
-            best = x0_sb[r]
-            for d in range(neighbours):
-                larger = held.tile([P, nodes], F32, name=f"larger{r}_{d}")
-                for h in range(halves):
-                    js = slice(h * HALF, (h + 1) * HALF)
-                    first = (d * nodes + h * HALF) // LANES
-                    picked = tab[r][:].indirect(offsets[:, first:first + HALF // LANES])
-                    nc.vector.tensor_tensor(larger[:, js], picked, best[:, js], MAX)
-                best = larger
+            last_block = r == r_blocks - 1
+            width = QUARTER if last_block else HALF
+            best = [x0_sb[r]] + [held.tile([P, nodes], F32, name=f"best{r}_{d}") for d in range(neighbours)]
+            for step in range(nodes // width + neighbours - 1):
+                for d in range(neighbours):
+                    j = (step - d) * width
+                    if 0 <= j < nodes:
+                        listed = offsets[:, (d * nodes + j) // LANES:(d * nodes + j + width) // LANES]
+                        nc.vector.tensor_tensor(best[d + 1][:, j:j + width], tab[r][:].indirect(listed),
+                                                best[d][:, j:j + width], MAX)
             x_bf = held.tile([P, nodes], BF16, name=f"x_bf{r}")
-            for h in range(halves):
-                js = slice(h * HALF, (h + 1) * HALF)
-                last = r == r_blocks - 1 and h == halves - 1
-                if last:
-                    nc.vector.tensor_copy(x_bf[:, js], best[:, js])
+            for j in range(0, nodes, width):
+                if last_block and j + width == nodes:
+                    nc.vector.tensor_copy(x_bf[:, j:j + width], best[-1][:, j:j + width])
                 else:
-                    nc.scalar.copy(x_bf[:, js], best[:, js])
+                    nc.scalar.copy(x_bf[:, j:j + width], best[-1][:, j:j + width])
+            for q, js in enumerate(quarters):
                 for m in range(m_blocks):
-                    nc.tensor.matmul(sums[h, m][:, :HALF], w_sb[:, r, m * P:(m + 1) * P], x_bf[:, js],
-                                     start=(r == 0), stop=(r == r_blocks - 1))
+                    nc.tensor.matmul(sums[q][m][:], w_sb[:, r, m * P:(m + 1) * P], x_bf[:, js],
+                                     start=(r == 0), stop=last_block)
 
-        for h in range(halves):
-            js = slice(h * HALF, (h + 1) * HALF)
+        out_rows = out.rearrange("(m p) j -> p m j", p=P)
+        for q, js in enumerate(quarters):
+            result = held.tile([P, m_blocks, QUARTER], F32, name=f"result{q}")
             for m in range(m_blocks):
-                result = held.tile([P, HALF], F32, name=f"result{h}_{m}")
-                if m % 2 == 1:
-                    nc.vector.tensor_scalar(result[:], sums[h, m][:, :HALF], bias[m][:], 0.0, ADD, MAX)
+                if m % 2 == 1 and q >= len(quarters) - 2:
+                    nc.vector.tensor_scalar(result[:, m, :], sums[q][m][:], bias[m][:], 0.0, ADD, MAX)
                 else:
-                    nc.scalar.activation(result[:], sums[h, m][:, :HALF], RELU, bias=bias[m][:])
-                nc.sync.dma_start(out_rows[:, m, js], result[:])
+                    nc.scalar.activation(result[:, m, :], sums[q][m][:], RELU, bias=bias[m][:])
+            nc.sync.dma_start(out_rows[:, :, js], result[:])

import concourse.mybir as mybir

BF16, F32, U16 = mybir.dt.bfloat16, mybir.dt.float32, mybir.dt.uint16
ADD, MAX = mybir.AluOpType.add, mybir.AluOpType.max
RELU = mybir.ActivationFunctionType.Relu

P = 128
BANK = 512
LANES = 16
HALF = 256
QUARTER = 128
WARM_UPS = 8

FLOPS = 2 * 256 * 256 * 2048 + 2 * 256 * 256 * 512


def tile_lookup_pjmax_relu_kernel(tc, z, wt, x0, w, b, offs, out):
    nc = tc.nc
    features, places = z.shape
    rows, nodes = x0.shape
    outputs = w.shape[1]
    k_blocks, r_blocks, m_blocks = features // P, rows // P, outputs // P
    starts = list(range(0, places - BANK, BANK)) + [places - BANK, places - BANK // 2]
    chunks = [slice(a, e) for a, e in zip(starts, starts[1:] + [places])]
    quarters = [slice(a, a + QUARTER) for a in range(0, nodes, QUARTER)]
    neighbours = offs.shape[1] * LANES // nodes

    with (
        tc.tile_pool(name="held", bufs=1) as held,
        tc.psum_pool(name="psum", bufs=8) as psum,
    ):
        offsets = held.tile([P, offs.shape[1]], U16, name="offsets")
        wt_sb = held.tile([P, k_blocks, rows], BF16, name="wt_sb")
        z_sb = [held.tile([P, k_blocks, cols.stop - cols.start], BF16, name=f"z{c}") for c, cols in enumerate(chunks)]
        x0_sb = [held.tile([P, nodes], F32, name=f"x0_{r}") for r in range(r_blocks)]
        w_sb = held.tile([P, r_blocks, outputs], BF16, name="w_sb")
        bias = [held.tile([P, 1], F32, name=f"bias{m}") for m in range(m_blocks)]

        z_rows = z.rearrange("(p k) i -> p k i", k=k_blocks)
        nc.sync.dma_start(wt_sb[:], wt.rearrange("(p k) r -> p k r", k=k_blocks))
        for c, cols in enumerate(chunks):
            nc.sync.dma_start(z_sb[c][:], z_rows[:, :, cols])
        nc.sync.dma_start(offsets[:], offs)
        for r in range(r_blocks):
            nc.sync.dma_start(x0_sb[r][:], x0[r * P:(r + 1) * P, :])
        nc.sync.dma_start(w_sb[:], w.rearrange("(r p) m -> p r m", p=P))
        for m in range(m_blocks):
            nc.sync.dma_start(bias[m][:], b[m * P:(m + 1) * P, :])

        zeros = held.tile([P, HALF], BF16, name="zeros")
        nc.vector.memset(zeros[:], 0.0)
        bank = psum.tile([P, BANK], F32, name="bank")
        for i in range(WARM_UPS):
            nc.tensor.matmul(bank[:, :HALF], zeros[:, :P], zeros[:], start=True, stop=True)

        tab = [held.tile([P, places], F32, name=f"tab{r}") for r in range(r_blocks)]
        for r in range(r_blocks):
            for c, cols in enumerate(chunks):
                bank = psum.tile([P, BANK], F32, name="bank")
                projected = bank[:, :cols.stop - cols.start]
                for k in range(k_blocks):
                    nc.tensor.matmul(projected, wt_sb[:, k, r * P:(r + 1) * P], z_sb[c][:, k, :],
                                     start=(k == 0), stop=(k == k_blocks - 1))
                if r == 0 and c % 2 == 0:
                    nc.vector.tensor_copy(tab[r][:, cols], projected)
                else:
                    nc.scalar.copy(tab[r][:, cols], projected)

        sums = [[psum.tile([P, QUARTER], F32, name="bank") for m in range(m_blocks)] for js in quarters]
        for r in range(r_blocks):
            last_block = r == r_blocks - 1
            width = QUARTER if last_block else HALF
            best = [x0_sb[r]] + [held.tile([P, nodes], F32, name=f"best{r}_{d}") for d in range(neighbours)]
            for step in range(nodes // width + neighbours - 1):
                for d in range(neighbours):
                    j = (step - d) * width
                    if 0 <= j < nodes:
                        listed = offsets[:, (d * nodes + j) // LANES:(d * nodes + j + width) // LANES]
                        nc.vector.tensor_tensor(best[d + 1][:, j:j + width], tab[r][:].indirect(listed),
                                                best[d][:, j:j + width], MAX)
            x_bf = held.tile([P, nodes], BF16, name=f"x_bf{r}")
            for j in range(0, nodes, width):
                if last_block and j + width == nodes:
                    nc.vector.tensor_copy(x_bf[:, j:j + width], best[-1][:, j:j + width])
                else:
                    nc.scalar.copy(x_bf[:, j:j + width], best[-1][:, j:j + width])
            for q, js in enumerate(quarters):
                for m in range(m_blocks):
                    nc.tensor.matmul(sums[q][m][:], w_sb[:, r, m * P:(m + 1) * P], x_bf[:, js],
                                     start=(r == 0), stop=last_block)

        out_rows = out.rearrange("(m p) j -> p m j", p=P)
        for q, js in enumerate(quarters):
            result = held.tile([P, m_blocks, QUARTER], F32, name=f"result{q}")
            for m in range(m_blocks):
                if m % 2 == 1 and q >= len(quarters) - 2:
                    nc.vector.tensor_scalar(result[:, m, :], sums[q][m][:], bias[m][:], 0.0, ADD, MAX)
                else:
                    nc.scalar.activation(result[:, m, :], sums[q][m][:], RELU, bias=bias[m][:])
            nc.sync.dma_start(out_rows[:, :, js], result[:])
